import numpy as np
import ml_dtypes


def mxq(x, axis, fmt="e4m3"):
    dtype, down = {"e4m3": (ml_dtypes.float8_e4m3fn, 7), "e5m2": (ml_dtypes.float8_e5m2, 14)}[fmt]
    v = np.moveaxis(np.asarray(x, np.float32).astype(ml_dtypes.bfloat16).astype(np.float64), axis, -1)
    blocks = v.reshape(v.shape[:-1] + (-1, 32))
    amax = np.abs(blocks).max(-1, keepdims=True)
    byte = np.maximum(np.where(amax > 0, np.frexp(amax)[1] - 1 + 127, 0) - down, 1)
    scale = np.exp2(byte - 127.0)
    codes = (blocks / scale).astype(np.float32).astype(dtype).astype(np.float64)
    return np.moveaxis((codes * scale).reshape(v.shape), -1, axis)


WIDE = False


def mx_kscale(k):
    if not WIDE:
        return np.ones(k)
    levels = np.array([10, -10, 5, -5, 0])
    if k % 512:
        return np.exp2(np.random.permutation(np.resize(levels, k // 32))).repeat(32)
    a = np.empty((k // 512, 16))
    for p in range(k // 512):
        a[p, :8] = np.random.permutation(np.resize(levels, 8))
        for g in range(8):
            far = levels[np.abs(levels - a[p, g]) >= 10]
            a[p, g + 8] = far[np.random.randint(len(far))]
    return np.exp2(a.ravel()).repeat(32)


def f64(x):
    return np.asarray(x).astype(np.float64)


def striped(idx):
    return np.tile(idx.reshape(-1, 16).T, (8, 1)).astype(np.uint16)


def unstriped(offs):
    return offs[:16].T.reshape(-1).astype(np.int64)


def pack_weight(w):
    k, n = w.shape
    w = f64(np.asarray(w, np.float32).astype(ml_dtypes.bfloat16)).reshape(k // 32, 32, n)
    amax = np.abs(w).max(1)
    byte = np.clip(np.where(amax > 0, np.frexp(amax)[1] - 1 + 127 - 7, 1), 1, 254)
    scaled = (w * np.exp2(127.0 - byte)[:, None, :]).reshape(k, n).astype(np.float32)
    words = np.ascontiguousarray(scaled.reshape(k // 512, 128, 4, n).transpose(0, 1, 3, 2)).astype(ml_dtypes.float8_e4m3fn).view(np.uint8)
    return words, np.ascontiguousarray(byte.astype(np.uint8).reshape(k // 512, 16, n))


def unpack_weight(words, scales):
    g, p, n, _ = words.shape
    vals = np.ascontiguousarray(words).view(ml_dtypes.float8_e4m3fn).astype(np.float64) * np.repeat(np.exp2(scales.astype(np.float64) - 127.0), 8, axis=1)[..., None]
    return vals.transpose(0, 1, 3, 2).reshape(g * 512, n)


def sigmoid(v):
    return 1.0 / (1.0 + np.exp(-np.maximum(v, -700.0)))


K, T, S, N, U = 1024, 2048, 512, 256, 1024
P = 2 ** 7


def setup_inputs():
    n = np.random.standard_normal
    s = mx_kscale(K)[:, None]
    packed_xT = pack_weight(n((K, T)) * s)
    return {
        "x_words": packed_xT[0],
        "x_scales": packed_xT[1],
        "w1": (n((K, N)) / np.sqrt(K) / s).astype(np.float32),
        "w2": (n((K, N)) / np.sqrt(K) / s).astype(np.float32),
        "buf": (n((N, U))).astype(np.float32),
        "sent": (np.tile((np.random.uniform(size=S) < 0.8) * 1.0, (P, 1))).astype(np.float32),
        "lim": (np.tile(np.random.uniform(1.0, 2.5, S), (P, 1))).astype(np.float32),
        "offs": striped(np.random.permutation(T)[:S]),
        "slot": striped(np.random.permutation(U)[:S]),
    }


def reference(x_words, x_scales, w1, w2, buf, sent, lim, offs, slot):
    bufg = f64(buf)[:, unstriped(slot)]
    xq = unpack_weight(x_words, x_scales)[:, unstriped(offs)]
    yr = mxq(f64(w1), 0, "e4m3").T @ xq
    yg = mxq(f64(w2), 0, "e4m3").T @ xq
    gain = sigmoid(yg)
    llr = 2.0 * ((yr * gain) / (-1.0 * gain + 1.2))
    comb = bufg + f64(sent)[:1] * llr
    cclip = np.maximum(np.minimum(comb, f64(lim)[:1]), -1.0 * f64(lim)[:1])
    out = f64(buf).copy()
    out[:, unstriped(slot)] = cclip
    return out

@@ -1,0 +1,181 @@
+import math
+from contextlib import ExitStack
+
+import concourse.mybir as mybir
+from concourse.masks import make_identity
+
+K, T, S, N, U = 1024, 2048, 512, 256, 1024
+FLOPS = 2 * 2 * K * N * S
+
+F32 = mybir.dt.float32
+BF16 = mybir.dt.bfloat16
+I32 = mybir.dt.int32
+U32 = mybir.dt.uint32
+U16 = mybir.dt.uint16
+U8 = mybir.dt.uint8
+FP8X4 = mybir.dt.float8_e4m3fn_x4
+ALU = mybir.AluOpType
+ACT = mybir.ActivationFunctionType
+
+P = 128
+PACK = 4
+PASSES = K // (P * PACK)
+BLOCKS = S // P
+HALVES = N // P
+PART = S // 2
+PER_COL = 16
+
+
+def tile_picked_yharq_put_p_kernel(
+    tc, x_words, x_scales, w1, w2, buf, sent, lim, offs, slot, out
+):
+    nc = tc.nc
+    with ExitStack() as ctx:
+        keep = ctx.enter_context(tc.tile_pool(name="keep", bufs=1))
+        psum = ctx.enter_context(tc.psum_pool(name="psum", bufs=1))
+
+        offs_t = keep.tile([P, S // PER_COL], U16, name="offs_t")
+        slot_t = keep.tile([P, S // PER_COL], U16, name="slot_t")
+        planes = keep.tile([P, T], U8, name="planes", align_bytes=64)
+        rows = keep.tile([P, P], F32, name="rows")
+        ident = keep.tile([P, P], F32, name="ident")
+        warm = keep.tile([P, 1], F32, name="warm")
+        warm_out = keep.tile([P, 1], F32, name="warm_out")
+        w_raw = [keep.tile([P, PASSES, PACK, N], F32, name=f"w_raw{i}") for i in range(2)]
+        table = [keep.tile([P, T], U32, name=f"table{g}", align_bytes=64) for g in range(PASSES)]
+        window = [keep.tile([P, U], F32, name=f"window{h}", align_bytes=64) for h in range(HALVES)]
+
+        nc.vector.memset(planes[:].bitcast(I32), 0)
+        nc.gpsimd.memset(rows[:], 0.0)
+        nc.gpsimd.memset(warm[:], 0.0)
+        make_identity(nc, ident[:])
+        nc.scalar.activation(warm_out[:], warm[:], ACT.Sigmoid)
+
+        def load_w(i, w):
+            nc.sync.dma_start(w_raw[i][:], w.rearrange("(g p j) n -> p g j n", g=PASSES, j=PACK))
+
+        def load_table(g):
+            nc.sync.dma_start(
+                table[g][:].bitcast(I32), x_words[g].rearrange("p c r -> p (c r)").bitcast(I32)
+            )
+
+        load_w(0, w1)
+        for q in range(4):
+            nc.sync.dma_start(
+                planes[32 * q : 32 * q + 4 * PASSES, :].bitcast(I32),
+                x_scales[:, 4 * q : 4 * q + 4, :].bitcast(I32),
+            )
+        nc.sync.dma_start(rows[0:BLOCKS, :], sent[0, :].rearrange("(b c) -> b c", b=BLOCKS))
+        nc.sync.dma_start(rows[BLOCKS : 2 * BLOCKS, :], lim[0, :].rearrange("(b c) -> b c", b=BLOCKS))
+        load_w(1, w2)
+        nc.sync.dma_start(offs_t[:], offs)
+        load_table(0)
+        load_table(1)
+        nc.sync.dma_start(slot_t[:], slot)
+        for h in range(HALVES):
+            nc.sync.dma_start(window[h][:], buf[h * P : (h + 1) * P, :])
+
+        w_codes = [keep.tile([P, 2 * N], U32, name=f"w_codes{g}", align_bytes=64) for g in range(PASSES)]
+        w_scales = [keep.tile([P, 2 * N], U8, name=f"w_scales{g}", align_bytes=64) for g in range(PASSES)]
+        x_plane = keep.tile([P, S], U8, name="x_plane", align_bytes=64)
+
+        def quantise_w(i):
+            grouped = [keep.tile([P, N, PACK], BF16, name=f"grouped{i}{g}", align_bytes=64) for g in range(PASSES)]
+            nc.vector.tensor_copy(grouped[0][:], w_raw[i][:, 0].rearrange("p j n -> p n j"))
+            nc.scalar.copy(grouped[1][:], w_raw[i][:, 1].rearrange("p j n -> p n j"))
+            for g in range(PASSES):
+                nc.vector.quantize_mx(
+                    out=w_codes[g][:, i * N : (i + 1) * N].bitcast(FP8X4),
+                    scales=w_scales[g][:, i * N : (i + 1) * N],
+                    in_=grouped[g][:].rearrange("p n j -> p (n j)"),
+                )
+
+        quantise_w(0)
+        nc.vector.tensor_copy(x_plane[:], planes[:].indirect(offs_t[:]))
+
+        cols_ps = psum.tile([P, P], F32, name="cols_ps", tag="sum00")
+        nc.tensor.transpose(cols_ps[:], rows[:], ident[:])
+        sent10 = keep.tile([P, BLOCKS], F32, name="sent10")
+        lim_col = keep.tile([P, BLOCKS], F32, name="lim_col")
+        nc.vector.tensor_scalar(sent10[:], cols_ps[:, 0:BLOCKS], 10.0, None, ALU.mult)
+        nc.vector.tensor_copy(lim_col[:], cols_ps[:, BLOCKS : 2 * BLOCKS])
+
+        def spread_lim(dst, b, start, stop):
+            nc.tensor.matmul(
+                dst, lim_col[:, b : b + 1].to_broadcast([P, P]), ident[:], start=start, stop=stop, is_transpose=True
+            )
+
+        lim_ps = psum.tile([P, S], F32, name="lim_ps", tag="sum01")
+        for b in range(BLOCKS):
+            spread_lim(lim_ps[:, b * P : (b + 1) * P], b, True, True)
+        cap = keep.tile([P, S], F32, name="cap")
+        neg_lim = keep.tile([P, S], F32, name="neg_lim")
+        nc.scalar.activation(cap[:], lim_ps[:], ACT.Relu, scale=2.0)
+        nc.scalar.activation(neg_lim[:], lim_ps[:], ACT.Copy, scale=-1.0)
+
+        quantise_w(1)
+
+        sums = {}
+        for h in range(HALVES):
+            for u in range(2):
+                sums[h, u] = psum.tile([P, PART], F32, name=f"sum{h}{u}", tag=f"sum{h}{u}")
+                for i in range(2):
+                    spread_lim(sums[h, u][:, i * P : (i + 1) * P], 2 * u + i, i == 0, False)
+
+        acc = [psum.tile([P, 2 * N], F32, name=f"acc{b}") for b in range(BLOCKS)]
+        for g in range(PASSES):
+            for u in range(2):
+                picked = keep.tile([P, PART], U32, name=f"picked{g}{u}", align_bytes=64)
+                cols = slice(u * PART // PER_COL, (u + 1) * PART // PER_COL)
+                nc.vector.tensor_copy(picked[:], table[g][:].indirect(offs_t[:, cols]))
+                for i in range(2):
+                    b = 2 * u + i
+                    nc.tensor.matmul_mx(
+                        out=acc[b][:],
+                        lhsT=picked[:, i * P : (i + 1) * P].bitcast(FP8X4),
+                        lhsT_scale=x_plane[4 * g : P, b * P : (b + 1) * P],
+                        rhs=w_codes[g][:].bitcast(FP8X4),
+                        rhs_scale=w_scales[g][:],
+                        start=(g == 0),
+                        stop=(g == PASSES - 1),
+                    )
+
+        shifted = {}
+        for u in range(2):
+            for i in range(2):
+                b = 2 * u + i
+                gain = keep.tile([P, N], F32, name=f"gain{b}")
+                llr = keep.tile([P, N], F32, name=f"llr{b}")
+                nc.scalar.activation(gain[:], acc[b][:, N : 2 * N], ACT.Sigmoid, bias=-math.log(6.0))
+                nc.vector.scalar_tensor_tensor(
+                    llr[:], acc[b][:, 0:N], sent10[:, b : b + 1], gain[:], ALU.mult, ALU.mult
+                )
+                for h in range(HALVES):
+                    nc.tensor.matmul(
+                        sums[h, u][:, i * P : (i + 1) * P],
+                        llr[:, h * P : (h + 1) * P],
+                        ident[:],
+                        start=False,
+                        stop=(i == 1),
+                        is_transpose=True,
+                    )
+            for h in range(HALVES):
+                shifted[h, u] = keep.tile([P, PART], F32, name=f"shifted{h}{u}")
+                nc.scalar.copy(shifted[h, u][:], sums[h, u][:])
+
+        comb = [keep.tile([P, S], F32, name=f"comb{h}") for h in range(HALVES)]
+        for u in range(2):
+            cols = slice(u * PART // PER_COL, (u + 1) * PART // PER_COL)
+            for h in range(HALVES):
+                nc.vector.tensor_tensor(
+                    comb[h][:, u * PART : (u + 1) * PART],
+                    window[h][:].indirect(slot_t[:, cols]),
+                    shifted[h, u][:],
+                    ALU.add,
+                )
+        clipped = [keep.tile([P, S], F32, name=f"clipped{h}") for h in range(HALVES)]
+        for h in range(HALVES):
+            nc.vector.scalar_tensor_tensor(clipped[h][:], comb[h][:], 0.0, cap[:], ALU.max, ALU.min)
+        for h in range(HALVES):
+            nc.vector.tensor_tensor(window[h][:].indirect(slot_t[:]), clipped[h][:], neg_lim[:], ALU.add)
+            nc.sync.dma_start(out[h * P : (h + 1) * P, :], window[h][:])

@@ -24,6 +24,7 @@ BLOCKS = S // P
 HALVES = N // P
 PART = S // 2
 PER_COL = 16
+KIB = 1024
 
 
 def tile_picked_yharq_put_p_kernel(
@@ -32,6 +33,7 @@ def tile_picked_yharq_put_p_kernel(
     nc = tc.nc
     with ExitStack() as ctx:
         keep = ctx.enter_context(tc.tile_pool(name="keep", bufs=1))
+        reuse = ctx.enter_context(tc.tile_pool(name="reuse", bufs=1))
         psum = ctx.enter_context(tc.psum_pool(name="psum", bufs=1))
 
         offs_t = keep.tile([P, S // PER_COL], U16, name="offs_t")
@@ -40,112 +42,128 @@ def tile_picked_yharq_put_p_kernel(
         rows = keep.tile([P, P], F32, name="rows")
         ident = keep.tile([P, P], F32, name="ident")
         warm = keep.tile([P, 1], F32, name="warm")
-        warm_out = keep.tile([P, 1], F32, name="warm_out")
-        w_raw = [keep.tile([P, PASSES, PACK, N], F32, name=f"w_raw{i}") for i in range(2)]
+        gains = [keep.tile([P, N], F32, name=f"gain{b}") for b in range(BLOCKS)]
+        w_raw = [[keep.tile([P, PACK, N], F32, name=f"w_raw{g}{i}") for i in range(2)] for g in range(PASSES)]
         table = [keep.tile([P, T], U32, name=f"table{g}", align_bytes=64) for g in range(PASSES)]
         window = [keep.tile([P, U], F32, name=f"window{h}", align_bytes=64) for h in range(HALVES)]
 
         nc.vector.memset(planes[:].bitcast(I32), 0)
-        nc.gpsimd.memset(rows[:], 0.0)
+        nc.vector.memset(rows[:], 0.0)
         nc.gpsimd.memset(warm[:], 0.0)
         make_identity(nc, ident[:])
-        nc.scalar.activation(warm_out[:], warm[:], ACT.Sigmoid)
-
-        def load_w(i, w):
-            nc.sync.dma_start(w_raw[i][:], w.rearrange("(g p j) n -> p g j n", g=PASSES, j=PACK))
+        nc.scalar.activation(gains[0][:, 0:1], warm[:], ACT.Sigmoid)
 
         def load_table(g):
             nc.sync.dma_start(
                 table[g][:].bitcast(I32), x_words[g].rearrange("p c r -> p (c r)").bitcast(I32)
             )
 
-        load_w(0, w1)
+        def load_w(g):
+            for i, w in enumerate((w1, w2)):
+                nc.sync.dma_start(
+                    w_raw[g][i][:], w[g * P * PACK : (g + 1) * P * PACK, :].rearrange("(p j) n -> p j n", j=PACK)
+                )
+
+        load_table(0)
         for q in range(4):
             nc.sync.dma_start(
                 planes[32 * q : 32 * q + 4 * PASSES, :].bitcast(I32),
                 x_scales[:, 4 * q : 4 * q + 4, :].bitcast(I32),
             )
+        nc.sync.dma_start(offs_t[:], offs)
+        load_w(0)
         nc.sync.dma_start(rows[0:BLOCKS, :], sent[0, :].rearrange("(b c) -> b c", b=BLOCKS))
         nc.sync.dma_start(rows[BLOCKS : 2 * BLOCKS, :], lim[0, :].rearrange("(b c) -> b c", b=BLOCKS))
-        load_w(1, w2)
-        nc.sync.dma_start(offs_t[:], offs)
-        load_table(0)
+        load_w(1)
         load_table(1)
         nc.sync.dma_start(slot_t[:], slot)
-        for h in range(HALVES):
-            nc.sync.dma_start(window[h][:], buf[h * P : (h + 1) * P, :])
+        lim_t = keep.tile([P, S], F32, name="lim_t")
+        nc.sync.dma_start(window[0][:], buf[0:P, :])
+        nc.sync.dma_start(lim_t[:], lim)
+        nc.sync.dma_start(window[1][:], buf[P : 2 * P, :])
 
         w_codes = [keep.tile([P, 2 * N], U32, name=f"w_codes{g}", align_bytes=64) for g in range(PASSES)]
         w_scales = [keep.tile([P, 2 * N], U8, name=f"w_scales{g}", align_bytes=64) for g in range(PASSES)]
         x_plane = keep.tile([P, S], U8, name="x_plane", align_bytes=64)
 
-        def quantise_w(i):
-            grouped = [keep.tile([P, N, PACK], BF16, name=f"grouped{i}{g}", align_bytes=64) for g in range(PASSES)]
-            nc.vector.tensor_copy(grouped[0][:], w_raw[i][:, 0].rearrange("p j n -> p n j"))
-            nc.scalar.copy(grouped[1][:], w_raw[i][:, 1].rearrange("p j n -> p n j"))
-            for g in range(PASSES):
-                nc.vector.quantize_mx(
-                    out=w_codes[g][:, i * N : (i + 1) * N].bitcast(FP8X4),
-                    scales=w_scales[g][:, i * N : (i + 1) * N],
-                    in_=grouped[g][:].rearrange("p n j -> p (n j)"),
-                )
+        grouped = [
+            reuse.tile([P, 2 * N, PACK], BF16, name=f"grouped{g}", align_bytes=64, offset=g * 2 * N * PACK * 2)
+            for g in range(PASSES)
+        ]
 
-        quantise_w(0)
+        def quantise_w(g):
+            nc.scalar.copy(grouped[g][:, 0:N, :], w_raw[g][0][:].rearrange("p j n -> p n j"))
+            nc.vector.tensor_copy(grouped[g][:, N : 2 * N, :], w_raw[g][1][:].rearrange("p j n -> p n j"))
+            nc.vector.quantize_mx(
+                out=w_codes[g][:].bitcast(FP8X4),
+                scales=w_scales[g][:],
+                in_=grouped[g][:].rearrange("p n j -> p (n j)"),
+            )
+
+        def pick(g, u, picked):
+            cols = slice(u * PART // PER_COL, (u + 1) * PART // PER_COL)
+            nc.vector.tensor_copy(picked, table[g][:].indirect(offs_t[:, cols]))
+
+        picked0 = keep.tile([P, S], U32, name="picked0", align_bytes=64)
+        nc.vector.tensor_copy(picked0[:], table[0][:].indirect(offs_t[:]))
         nc.vector.tensor_copy(x_plane[:], planes[:].indirect(offs_t[:]))
 
-        cols_ps = psum.tile([P, P], F32, name="cols_ps", tag="sum00")
+        cols_ps = psum.tile([P, P], F32, name="cols_ps", tag="sum10")
         nc.tensor.transpose(cols_ps[:], rows[:], ident[:])
         sent10 = keep.tile([P, BLOCKS], F32, name="sent10")
         lim_col = keep.tile([P, BLOCKS], F32, name="lim_col")
-        nc.vector.tensor_scalar(sent10[:], cols_ps[:, 0:BLOCKS], 10.0, None, ALU.mult)
-        nc.vector.tensor_copy(lim_col[:], cols_ps[:, BLOCKS : 2 * BLOCKS])
-
-        def spread_lim(dst, b, start, stop):
-            nc.tensor.matmul(
-                dst, lim_col[:, b : b + 1].to_broadcast([P, P]), ident[:], start=start, stop=stop, is_transpose=True
-            )
-
-        lim_ps = psum.tile([P, S], F32, name="lim_ps", tag="sum01")
-        for b in range(BLOCKS):
-            spread_lim(lim_ps[:, b * P : (b + 1) * P], b, True, True)
-        cap = keep.tile([P, S], F32, name="cap")
-        neg_lim = keep.tile([P, S], F32, name="neg_lim")
-        nc.scalar.activation(cap[:], lim_ps[:], ACT.Relu, scale=2.0)
-        nc.scalar.activation(neg_lim[:], lim_ps[:], ACT.Copy, scale=-1.0)
-
-        quantise_w(1)
+        cap_col = keep.tile([P, BLOCKS], F32, name="cap_col")
+        nc.scalar.copy(lim_col[:], cols_ps[:, BLOCKS : 2 * BLOCKS])
+        nc.scalar.activation(sent10[:], cols_ps[:, 0:BLOCKS], ACT.Copy, scale=10.0)
+        nc.scalar.activation(cap_col[:], cols_ps[:, BLOCKS : 2 * BLOCKS], ACT.Relu, scale=2.0)
 
         sums = {}
         for h in range(HALVES):
             for u in range(2):
                 sums[h, u] = psum.tile([P, PART], F32, name=f"sum{h}{u}", tag=f"sum{h}{u}")
-                for i in range(2):
-                    spread_lim(sums[h, u][:, i * P : (i + 1) * P], 2 * u + i, i == 0, False)
+        for u in range(2):
+            for i in range(2):
+                b = 2 * u + i
+                nc.tensor.matmul(
+                    sums[0, u][:, i * P : (i + 1) * P],
+                    lim_col[:, b : b + 1].to_broadcast([P, P]),
+                    ident[:],
+                    start=(i == 0),
+                    stop=False,
+                    is_transpose=True,
+                )
 
-        acc = [psum.tile([P, 2 * N], F32, name=f"acc{b}") for b in range(BLOCKS)]
-        for g in range(PASSES):
-            for u in range(2):
-                picked = keep.tile([P, PART], U32, name=f"picked{g}{u}", align_bytes=64)
-                cols = slice(u * PART // PER_COL, (u + 1) * PART // PER_COL)
-                nc.vector.tensor_copy(picked[:], table[g][:].indirect(offs_t[:, cols]))
-                for i in range(2):
-                    b = 2 * u + i
-                    nc.tensor.matmul_mx(
-                        out=acc[b][:],
-                        lhsT=picked[:, i * P : (i + 1) * P].bitcast(FP8X4),
-                        lhsT_scale=x_plane[4 * g : P, b * P : (b + 1) * P],
-                        rhs=w_codes[g][:].bitcast(FP8X4),
-                        rhs_scale=w_scales[g][:],
-                        start=(g == 0),
-                        stop=(g == PASSES - 1),
-                    )
+        acc = [psum.tile([P, 2 * N], F32, name=f"acc{b}", tag=f"acc{b}") for b in range(BLOCKS)]
+
+        def product(g, b, words):
+            nc.tensor.matmul_mx(
+                out=acc[b][:],
+                lhsT=words.bitcast(FP8X4),
+                lhsT_scale=x_plane[4 * g : P, b * P : (b + 1) * P],
+                rhs=w_codes[g][:].bitcast(FP8X4),
+                rhs_scale=w_scales[g][:],
+                start=(g == 0),
+                stop=(g == PASSES - 1),
+            )
+
+        quantise_w(0)
+        for b in range(BLOCKS):
+            product(0, b, picked0[:, b * P : (b + 1) * P])
+        quantise_w(1)
+        for u in range(2):
+            picked = reuse.tile(
+                [P, PART], U32, name=f"picked1{u}", align_bytes=64, offset=2 * N * PACK * 2 + u * PART * 4
+            )
+            pick(1, u, picked[:])
+            for i in range(2):
+                product(1, 2 * u + i, picked[:, i * P : (i + 1) * P])
 
         shifted = {}
         for u in range(2):
             for i in range(2):
                 b = 2 * u + i
-                gain = keep.tile([P, N], F32, name=f"gain{b}")
-                llr = keep.tile([P, N], F32, name=f"llr{b}")
+                gain = gains[b]
+                llr = reuse.tile([P, N], F32, name=f"llr{b}", offset=8 * KIB + b * KIB)
                 nc.scalar.activation(gain[:], acc[b][:, N : 2 * N], ACT.Sigmoid, bias=-math.log(6.0))
                 nc.vector.scalar_tensor_tensor(
                     llr[:], acc[b][:, 0:N], sent10[:, b : b + 1], gain[:], ALU.mult, ALU.mult
@@ -155,27 +173,52 @@ def tile_picked_yharq_put_p_kernel(
                         sums[h, u][:, i * P : (i + 1) * P],
                         llr[:, h * P : (h + 1) * P],
                         ident[:],
-                        start=False,
-                        stop=(i == 1),
+                        start=(h == 1),
+                        stop=(h == 1 or i == 1),
                         is_transpose=True,
                     )
             for h in range(HALVES):
-                shifted[h, u] = keep.tile([P, PART], F32, name=f"shifted{h}{u}")
+                shifted[h, u] = reuse.tile([P, PART], F32, name=f"shifted{h}{u}", offset=12 * KIB + (2 * u + h) * KIB)
                 nc.scalar.copy(shifted[h, u][:], sums[h, u][:])
 
-        comb = [keep.tile([P, S], F32, name=f"comb{h}") for h in range(HALVES)]
+        neg_lim = reuse.tile([P, S], F32, name="neg_lim", offset=8 * KIB)
+        nc.scalar.activation(neg_lim[:], lim_t[:], ACT.Copy, scale=-1.0)
+        cap = reuse.tile([P, S], F32, name="cap", offset=10 * KIB)
+        nc.scalar.activation(cap[:], lim_t[:], ACT.Relu, scale=2.0)
+
+        comb0 = keep.tile([P, S], F32, name="comb0")
+        under = keep.tile([P, BLOCKS, P], F32, name="under")
+        under_ps = psum.tile([P, S], F32, name="under_ps", tag="acc2")
         for u in range(2):
             cols = slice(u * PART // PER_COL, (u + 1) * PART // PER_COL)
-            for h in range(HALVES):
-                nc.vector.tensor_tensor(
-                    comb[h][:, u * PART : (u + 1) * PART],
-                    window[h][:].indirect(slot_t[:, cols]),
-                    shifted[h, u][:],
-                    ALU.add,
+            comb1 = keep.tile([P, PART], F32, name=f"comb1{u}")
+            nc.vector.tensor_tensor(
+                comb0[:, u * PART : (u + 1) * PART], window[0][:].indirect(slot_t[:, cols]), shifted[0, u][:], ALU.add
+            )
+            nc.vector.tensor_tensor(comb1[:], window[1][:].indirect(slot_t[:, cols]), shifted[1, u][:], ALU.add)
+            turned = psum.tile([P, PART], F32, name=f"turned{u}", tag=f"acc{u}")
+            above = keep.tile([P, 2, P], F32, name=f"above{u}")
+            for i in range(2):
+                nc.tensor.transpose(turned[:, i * P : (i + 1) * P], comb1[:, i * P : (i + 1) * P], ident[:])
+            for i in range(2):
+                b = 2 * u + i
+                nc.scalar.activation(
+                    above[:, i, :], turned[:, i * P : (i + 1) * P], ACT.Relu, bias=lim_col[:, b : b + 1]
                 )
-        clipped = [keep.tile([P, S], F32, name=f"clipped{h}") for h in range(HALVES)]
-        for h in range(HALVES):
-            nc.vector.scalar_tensor_tensor(clipped[h][:], comb[h][:], 0.0, cap[:], ALU.max, ALU.min)
-        for h in range(HALVES):
-            nc.vector.tensor_tensor(window[h][:].indirect(slot_t[:]), clipped[h][:], neg_lim[:], ALU.add)
-            nc.sync.dma_start(out[h * P : (h + 1) * P, :], window[h][:])
+            for i in range(2):
+                b = 2 * u + i
+                nc.scalar.activation(
+                    under[:, b, :], above[:, i, :], ACT.Relu, bias=cap_col[:, b : b + 1], scale=-1.0
+                )
+                nc.tensor.transpose(under_ps[:, b * P : (b + 1) * P], under[:, b, :], ident[:])
+        abs_lim = reuse.tile([P, S], F32, name="abs_lim", offset=14 * KIB)
+        nc.scalar.activation(abs_lim[:], lim_t[:], ACT.Abs)
+        neg_under = keep.tile([P, S], F32, name="neg_under")
+        nc.scalar.activation(neg_under[:], under_ps[:], ACT.Copy, scale=-1.0)
+
+        clipped = keep.tile([P, S], F32, name="clipped")
+        nc.vector.scalar_tensor_tensor(clipped[:], comb0[:], 0.0, cap[:], ALU.max, ALU.min)
+        nc.vector.tensor_tensor(window[0][:].indirect(slot_t[:]), clipped[:], neg_lim[:], ALU.add)
+        nc.sync.dma_start(out[0:P, :], window[0][:])
+        nc.vector.tensor_tensor(window[1][:].indirect(slot_t[:]), neg_under[:], abs_lim[:], ALU.add)
+        nc.sync.dma_start(out[P : 2 * P, :], window[1][:])

@@ -20,11 +20,20 @@ ACT = mybir.ActivationFunctionType
 P = 128
 PACK = 4
 PASSES = K // (P * PACK)
+QUADRANT = 32
+SCALE_ROWS = 4
 BLOCKS = S // P
-HALVES = N // P
-PART = S // 2
+STREAM_TILES = N // P
+PARTS = 2
+PART = S // PARTS
+PART_BLOCKS = BLOCKS // PARTS
 PER_COL = 16
 KIB = 1024
+
+AT_GROUPED = 0
+AT_LLR = 8 * KIB
+AT_TURNED = 12 * KIB
+AT_LIM = 16 * KIB
 
 
 def tile_picked_yharq_put_p_kernel(
@@ -36,22 +45,25 @@ def tile_picked_yharq_put_p_kernel(
         reuse = ctx.enter_context(tc.tile_pool(name="reuse", bufs=1))
         psum = ctx.enter_context(tc.psum_pool(name="psum", bufs=1))
 
+        def block(b):
+            return slice(b * P, (b + 1) * P)
+
+        def list_part(u):
+            return slice(u * PART // PER_COL, (u + 1) * PART // PER_COL)
+
         offs_t = keep.tile([P, S // PER_COL], U16, name="offs_t")
         slot_t = keep.tile([P, S // PER_COL], U16, name="slot_t")
-        planes = keep.tile([P, T], U8, name="planes", align_bytes=64)
+        table_scales = keep.tile([P, T], U8, name="table_scales", align_bytes=64)
         rows = keep.tile([P, P], F32, name="rows")
         ident = keep.tile([P, P], F32, name="ident")
-        warm = keep.tile([P, 1], F32, name="warm")
-        gains = [keep.tile([P, N], F32, name=f"gain{b}") for b in range(BLOCKS)]
+        gain = [keep.tile([P, N], F32, name=f"gain{b}") for b in range(BLOCKS)]
         w_raw = [[keep.tile([P, PACK, N], F32, name=f"w_raw{g}{i}") for i in range(2)] for g in range(PASSES)]
         table = [keep.tile([P, T], U32, name=f"table{g}", align_bytes=64) for g in range(PASSES)]
-        window = [keep.tile([P, U], F32, name=f"window{h}", align_bytes=64) for h in range(HALVES)]
+        window = [keep.tile([P, U], F32, name=f"window{h}", align_bytes=64) for h in range(STREAM_TILES)]
 
-        nc.vector.memset(planes[:].bitcast(I32), 0)
+        nc.vector.memset(table_scales[:].bitcast(I32), 0)
         nc.vector.memset(rows[:], 0.0)
-        nc.gpsimd.memset(warm[:], 0.0)
         make_identity(nc, ident[:])
-        nc.scalar.activation(gains[0][:, 0:1], warm[:], ACT.Sigmoid)
 
         def load_table(g):
             nc.sync.dma_start(
@@ -65,10 +77,10 @@ def tile_picked_yharq_put_p_kernel(
                 )
 
         load_table(0)
-        for q in range(4):
+        for q in range(P // QUADRANT):
             nc.sync.dma_start(
-                planes[32 * q : 32 * q + 4 * PASSES, :].bitcast(I32),
-                x_scales[:, 4 * q : 4 * q + 4, :].bitcast(I32),
+                table_scales[QUADRANT * q : QUADRANT * q + SCALE_ROWS * PASSES, :].bitcast(I32),
+                x_scales[:, SCALE_ROWS * q : SCALE_ROWS * (q + 1), :].bitcast(I32),
             )
         nc.sync.dma_start(offs_t[:], offs)
         load_w(0)
@@ -77,17 +89,19 @@ def tile_picked_yharq_put_p_kernel(
         load_w(1)
         load_table(1)
         nc.sync.dma_start(slot_t[:], slot)
-        lim_t = keep.tile([P, S], F32, name="lim_t")
-        nc.sync.dma_start(window[0][:], buf[0:P, :])
+        lim_t = reuse.tile([P, S], F32, name="lim_t", offset=AT_LIM)
+        nc.sync.dma_start(window[0][:], buf[block(0), :])
         nc.sync.dma_start(lim_t[:], lim)
-        nc.sync.dma_start(window[1][:], buf[P : 2 * P, :])
+        nc.sync.dma_start(window[1][:], buf[block(1), :])
 
         w_codes = [keep.tile([P, 2 * N], U32, name=f"w_codes{g}", align_bytes=64) for g in range(PASSES)]
-        w_scales = [keep.tile([P, 2 * N], U8, name=f"w_scales{g}", align_bytes=64) for g in range(PASSES)]
-        x_plane = keep.tile([P, S], U8, name="x_plane", align_bytes=64)
-
+        w_scales = keep.tile([P, 2 * N], U8, name="w_scales", align_bytes=64)
+        x_picked_scales = keep.tile([P, S], U8, name="x_picked_scales", align_bytes=64)
+        grouped_bytes = 2 * N * PACK * 2
         grouped = [
-            reuse.tile([P, 2 * N, PACK], BF16, name=f"grouped{g}", align_bytes=64, offset=g * 2 * N * PACK * 2)
+            reuse.tile(
+                [P, 2 * N, PACK], BF16, name=f"grouped{g}", align_bytes=64, offset=AT_GROUPED + g * grouped_bytes
+            )
             for g in range(PASSES)
         ]
 
@@ -96,19 +110,15 @@ def tile_picked_yharq_put_p_kernel(
             nc.vector.tensor_copy(grouped[g][:, N : 2 * N, :], w_raw[g][1][:].rearrange("p j n -> p n j"))
             nc.vector.quantize_mx(
                 out=w_codes[g][:].bitcast(FP8X4),
-                scales=w_scales[g][:],
+                scales=w_scales[SCALE_ROWS * g : P, :],
                 in_=grouped[g][:].rearrange("p n j -> p (n j)"),
             )
 
-        def pick(g, u, picked):
-            cols = slice(u * PART // PER_COL, (u + 1) * PART // PER_COL)
-            nc.vector.tensor_copy(picked, table[g][:].indirect(offs_t[:, cols]))
-
         picked0 = keep.tile([P, S], U32, name="picked0", align_bytes=64)
         nc.vector.tensor_copy(picked0[:], table[0][:].indirect(offs_t[:]))
-        nc.vector.tensor_copy(x_plane[:], planes[:].indirect(offs_t[:]))
+        nc.vector.tensor_copy(x_picked_scales[:], table_scales[:].indirect(offs_t[:]))
 
-        cols_ps = psum.tile([P, P], F32, name="cols_ps", tag="sum10")
+        cols_ps = psum.tile([P, P], F32, name="cols_ps", tag="turned_ps10")
         nc.tensor.transpose(cols_ps[:], rows[:], ident[:])
         sent10 = keep.tile([P, BLOCKS], F32, name="sent10")
         lim_col = keep.tile([P, BLOCKS], F32, name="lim_col")
@@ -117,15 +127,15 @@ def tile_picked_yharq_put_p_kernel(
         nc.scalar.activation(sent10[:], cols_ps[:, 0:BLOCKS], ACT.Copy, scale=10.0)
         nc.scalar.activation(cap_col[:], cols_ps[:, BLOCKS : 2 * BLOCKS], ACT.Relu, scale=2.0)
 
-        sums = {}
-        for h in range(HALVES):
-            for u in range(2):
-                sums[h, u] = psum.tile([P, PART], F32, name=f"sum{h}{u}", tag=f"sum{h}{u}")
-        for u in range(2):
-            for i in range(2):
-                b = 2 * u + i
+        turned_ps = {}
+        for h in range(STREAM_TILES):
+            for u in range(PARTS):
+                turned_ps[h, u] = psum.tile([P, PART], F32, name=f"turned_ps{h}{u}", tag=f"turned_ps{h}{u}")
+        for u in range(PARTS):
+            for i in range(PART_BLOCKS):
+                b = PART_BLOCKS * u + i
                 nc.tensor.matmul(
-                    sums[0, u][:, i * P : (i + 1) * P],
+                    turned_ps[0, u][:, block(i)],
                     lim_col[:, b : b + 1].to_broadcast([P, P]),
                     ident[:],
                     start=(i == 0),
@@ -139,86 +149,91 @@ def tile_picked_yharq_put_p_kernel(
             nc.tensor.matmul_mx(
                 out=acc[b][:],
                 lhsT=words.bitcast(FP8X4),
-                lhsT_scale=x_plane[4 * g : P, b * P : (b + 1) * P],
+                lhsT_scale=x_picked_scales[SCALE_ROWS * g : P, block(b)],
                 rhs=w_codes[g][:].bitcast(FP8X4),
-                rhs_scale=w_scales[g][:],
+                rhs_scale=w_scales[SCALE_ROWS * g : P, :],
                 start=(g == 0),
                 stop=(g == PASSES - 1),
             )
 
         quantise_w(0)
-        for b in range(BLOCKS):
-            product(0, b, picked0[:, b * P : (b + 1) * P])
+        for b in range(PART_BLOCKS):
+            product(0, b, picked0[:, block(b)])
         quantise_w(1)
-        for u in range(2):
-            picked = reuse.tile(
-                [P, PART], U32, name=f"picked1{u}", align_bytes=64, offset=2 * N * PACK * 2 + u * PART * 4
+        for b in range(PART_BLOCKS, BLOCKS):
+            product(0, b, picked0[:, block(b)])
+        for u in range(PARTS):
+            picked1 = reuse.tile(
+                [P, PART], U32, name=f"picked1{u}", align_bytes=64, offset=AT_GROUPED + grouped_bytes + u * PART * 4
             )
-            pick(1, u, picked[:])
-            for i in range(2):
-                product(1, 2 * u + i, picked[:, i * P : (i + 1) * P])
+            nc.vector.tensor_copy(picked1[:], table[1][:].indirect(offs_t[:, list_part(u)]))
+            for i in range(PART_BLOCKS):
+                product(1, PART_BLOCKS * u + i, picked1[:, block(i)])
 
-        shifted = {}
-        for u in range(2):
-            for i in range(2):
-                b = 2 * u + i
-                gain = gains[b]
-                llr = reuse.tile([P, N], F32, name=f"llr{b}", offset=8 * KIB + b * KIB)
-                nc.scalar.activation(gain[:], acc[b][:, N : 2 * N], ACT.Sigmoid, bias=-math.log(6.0))
+        turned = {}
+        for u in range(PARTS):
+            llr = []
+            for i in range(PART_BLOCKS):
+                b = PART_BLOCKS * u + i
+                llr.append(reuse.tile([P, N], F32, name=f"llr{b}", offset=AT_LLR + b * KIB))
+                nc.scalar.activation(gain[b][:], acc[b][:, N : 2 * N], ACT.Sigmoid, bias=-math.log(6.0))
                 nc.vector.scalar_tensor_tensor(
-                    llr[:], acc[b][:, 0:N], sent10[:, b : b + 1], gain[:], ALU.mult, ALU.mult
+                    llr[i][:], acc[b][:, 0:N], sent10[:, b : b + 1], gain[b][:], ALU.mult, ALU.mult
                 )
-                for h in range(HALVES):
+            for h in range(STREAM_TILES):
+                onto_lim = h == 0
+                for i in range(PART_BLOCKS):
                     nc.tensor.matmul(
-                        sums[h, u][:, i * P : (i + 1) * P],
-                        llr[:, h * P : (h + 1) * P],
+                        turned_ps[h, u][:, block(i)],
+                        llr[i][:, block(h)],
                         ident[:],
-                        start=(h == 1),
-                        stop=(h == 1 or i == 1),
+                        start=not onto_lim,
+                        stop=not onto_lim or i == PART_BLOCKS - 1,
                         is_transpose=True,
                     )
-            for h in range(HALVES):
-                shifted[h, u] = reuse.tile([P, PART], F32, name=f"shifted{h}{u}", offset=12 * KIB + (2 * u + h) * KIB)
-                nc.scalar.copy(shifted[h, u][:], sums[h, u][:])
+                turned[h, u] = reuse.tile(
+                    [P, PART], F32, name=f"turned{h}{u}", offset=AT_TURNED + (STREAM_TILES * u + h) * KIB
+                )
+                nc.scalar.copy(turned[h, u][:], turned_ps[h, u][:])
 
-        neg_lim = reuse.tile([P, S], F32, name="neg_lim", offset=8 * KIB)
+        neg_lim = reuse.tile([P, S], F32, name="neg_lim", offset=AT_LLR)
         nc.scalar.activation(neg_lim[:], lim_t[:], ACT.Copy, scale=-1.0)
-        cap = reuse.tile([P, S], F32, name="cap", offset=10 * KIB)
+        cap = reuse.tile([P, S], F32, name="cap", offset=AT_LLR + PART_BLOCKS * KIB)
         nc.scalar.activation(cap[:], lim_t[:], ACT.Relu, scale=2.0)
 
         comb0 = keep.tile([P, S], F32, name="comb0")
         under = keep.tile([P, BLOCKS, P], F32, name="under")
         under_ps = psum.tile([P, S], F32, name="under_ps", tag="acc2")
-        for u in range(2):
-            cols = slice(u * PART // PER_COL, (u + 1) * PART // PER_COL)
+        for u in range(PARTS):
             comb1 = keep.tile([P, PART], F32, name=f"comb1{u}")
             nc.vector.tensor_tensor(
-                comb0[:, u * PART : (u + 1) * PART], window[0][:].indirect(slot_t[:, cols]), shifted[0, u][:], ALU.add
+                comb0[:, u * PART : (u + 1) * PART],
+                window[0][:].indirect(slot_t[:, list_part(u)]),
+                turned[0, u][:],
+                ALU.add,
             )
-            nc.vector.tensor_tensor(comb1[:], window[1][:].indirect(slot_t[:, cols]), shifted[1, u][:], ALU.add)
-            turned = psum.tile([P, PART], F32, name=f"turned{u}", tag=f"acc{u}")
-            above = keep.tile([P, 2, P], F32, name=f"above{u}")
-            for i in range(2):
-                nc.tensor.transpose(turned[:, i * P : (i + 1) * P], comb1[:, i * P : (i + 1) * P], ident[:])
-            for i in range(2):
-                b = 2 * u + i
-                nc.scalar.activation(
-                    above[:, i, :], turned[:, i * P : (i + 1) * P], ACT.Relu, bias=lim_col[:, b : b + 1]
-                )
-            for i in range(2):
-                b = 2 * u + i
+            nc.vector.tensor_tensor(comb1[:], window[1][:].indirect(slot_t[:, list_part(u)]), turned[1, u][:], ALU.add)
+            comb1_ps = psum.tile([P, PART], F32, name=f"comb1_ps{u}", tag=f"acc{u}")
+            above = reuse.tile([P, PART_BLOCKS, P], F32, name=f"above{u}", offset=AT_LIM + u * KIB)
+            for i in range(PART_BLOCKS):
+                nc.tensor.transpose(comb1_ps[:, block(i)], comb1[:, block(i)], ident[:])
+            for i in range(PART_BLOCKS):
+                b = PART_BLOCKS * u + i
+                nc.scalar.activation(above[:, i, :], comb1_ps[:, block(i)], ACT.Relu, bias=lim_col[:, b : b + 1])
+            for i in range(PART_BLOCKS):
+                b = PART_BLOCKS * u + i
                 nc.scalar.activation(
                     under[:, b, :], above[:, i, :], ACT.Relu, bias=cap_col[:, b : b + 1], scale=-1.0
                 )
-                nc.tensor.transpose(under_ps[:, b * P : (b + 1) * P], under[:, b, :], ident[:])
-        abs_lim = reuse.tile([P, S], F32, name="abs_lim", offset=14 * KIB)
-        nc.scalar.activation(abs_lim[:], lim_t[:], ACT.Abs)
+                nc.tensor.transpose(under_ps[:, block(b)], under[:, b, :], ident[:])
+        abs_lim = reuse.tile([P, S], F32, name="abs_lim", offset=AT_TURNED + STREAM_TILES * KIB)
+        nc.scalar.activation(abs_lim[:], neg_lim[:], ACT.Abs)
         neg_under = keep.tile([P, S], F32, name="neg_under")
         nc.scalar.activation(neg_under[:], under_ps[:], ACT.Copy, scale=-1.0)
 
-        clipped = keep.tile([P, S], F32, name="clipped")
-        nc.vector.scalar_tensor_tensor(clipped[:], comb0[:], 0.0, cap[:], ALU.max, ALU.min)
-        nc.vector.tensor_tensor(window[0][:].indirect(slot_t[:]), clipped[:], neg_lim[:], ALU.add)
-        nc.sync.dma_start(out[0:P, :], window[0][:])
+        capped0 = keep.tile([P, S], F32, name="capped0")
+        nc.vector.scalar_tensor_tensor(capped0[:], comb0[:], 0.0, cap[:], ALU.max, ALU.min)
+        nc.vector.tensor_tensor(window[0][:].indirect(slot_t[:]), capped0[:], neg_lim[:], ALU.add)
+        nc.sync.dma_start(out[block(0), :], window[0][:])
         nc.vector.tensor_tensor(window[1][:].indirect(slot_t[:]), neg_under[:], abs_lim[:], ALU.add)
-        nc.sync.dma_start(out[P : 2 * P, :], window[1][:])
+        nc.sync.dma_start(out[block(1), :], window[1][:])

@@ -28,12 +28,6 @@ PARTS = 2
 PART = S // PARTS
 PART_BLOCKS = BLOCKS // PARTS
 PER_COL = 16
-KIB = 1024
-
-AT_GROUPED = 0
-AT_LLR = 8 * KIB
-AT_TURNED = 12 * KIB
-AT_LIM = 16 * KIB
 
 
 def tile_picked_yharq_put_p_kernel(
@@ -57,66 +51,56 @@ def tile_picked_yharq_put_p_kernel(
         rows = keep.tile([P, P], F32, name="rows")
         ident = keep.tile([P, P], F32, name="ident")
         gain = [keep.tile([P, N], F32, name=f"gain{b}") for b in range(BLOCKS)]
-        w_raw = [[keep.tile([P, PACK, N], F32, name=f"w_raw{g}{i}") for i in range(2)] for g in range(PASSES)]
+        w_raw = [keep.tile([P, PASSES, PACK, N], F32, name=f"w_raw{i}") for i in range(2)]
         table = [keep.tile([P, T], U32, name=f"table{g}", align_bytes=64) for g in range(PASSES)]
         window = [keep.tile([P, U], F32, name=f"window{h}", align_bytes=64) for h in range(STREAM_TILES)]
 
         nc.vector.memset(table_scales[:].bitcast(I32), 0)
-        nc.vector.memset(rows[:], 0.0)
+        nc.gpsimd.memset(rows[:], 0.0)
         make_identity(nc, ident[:])
 
-        def load_table(g):
-            nc.sync.dma_start(
-                table[g][:].bitcast(I32), x_words[g].rearrange("p c r -> p (c r)").bitcast(I32)
-            )
+        def load_w(i, w):
+            nc.sync.dma_start(w_raw[i][:], w.rearrange("(g p j) n -> p g j n", g=PASSES, j=PACK))
 
-        def load_w(g):
-            for i, w in enumerate((w1, w2)):
-                nc.sync.dma_start(
-                    w_raw[g][i][:], w[g * P * PACK : (g + 1) * P * PACK, :].rearrange("(p j) n -> p j n", j=PACK)
-                )
-
-        load_table(0)
+        load_w(0, w1)
+        nc.sync.dma_start(offs_t[:], offs)
         for q in range(P // QUADRANT):
             nc.sync.dma_start(
                 table_scales[QUADRANT * q : QUADRANT * q + SCALE_ROWS * PASSES, :].bitcast(I32),
                 x_scales[:, SCALE_ROWS * q : SCALE_ROWS * (q + 1), :].bitcast(I32),
             )
-        nc.sync.dma_start(offs_t[:], offs)
-        load_w(0)
+        load_w(1, w2)
         nc.sync.dma_start(rows[0:BLOCKS, :], sent[0, :].rearrange("(b c) -> b c", b=BLOCKS))
         nc.sync.dma_start(rows[BLOCKS : 2 * BLOCKS, :], lim[0, :].rearrange("(b c) -> b c", b=BLOCKS))
-        load_w(1)
-        load_table(1)
+        for g in range(PASSES):
+            nc.sync.dma_start(table[g][:].bitcast(I32), x_words[g].rearrange("p c r -> p (c r)").bitcast(I32))
         nc.sync.dma_start(slot_t[:], slot)
-        lim_t = reuse.tile([P, S], F32, name="lim_t", offset=AT_LIM)
-        nc.sync.dma_start(window[0][:], buf[block(0), :])
-        nc.sync.dma_start(lim_t[:], lim)
-        nc.sync.dma_start(window[1][:], buf[block(1), :])
+        for h in range(STREAM_TILES):
+            nc.sync.dma_start(window[h][:], buf[block(h), :])
 
         w_codes = [keep.tile([P, 2 * N], U32, name=f"w_codes{g}", align_bytes=64) for g in range(PASSES)]
-        w_scales = keep.tile([P, 2 * N], U8, name="w_scales", align_bytes=64)
+        w_scales = [keep.tile([P, 2 * N], U8, name=f"w_scales{g}", align_bytes=64) for g in range(PASSES)]
         x_picked_scales = keep.tile([P, S], U8, name="x_picked_scales", align_bytes=64)
         grouped_bytes = 2 * N * PACK * 2
         grouped = [
-            reuse.tile(
-                [P, 2 * N, PACK], BF16, name=f"grouped{g}", align_bytes=64, offset=AT_GROUPED + g * grouped_bytes
-            )
+            reuse.tile([P, 2 * N, PACK], BF16, name=f"grouped{g}", align_bytes=64, offset=g * grouped_bytes)
             for g in range(PASSES)
         ]
 
-        def quantise_w(g):
-            nc.scalar.copy(grouped[g][:, 0:N, :], w_raw[g][0][:].rearrange("p j n -> p n j"))
-            nc.vector.tensor_copy(grouped[g][:, N : 2 * N, :], w_raw[g][1][:].rearrange("p j n -> p n j"))
-            nc.vector.quantize_mx(
-                out=w_codes[g][:].bitcast(FP8X4),
-                scales=w_scales[SCALE_ROWS * g : P, :],
-                in_=grouped[g][:].rearrange("p n j -> p (n j)"),
-            )
+        def quantise_w(i):
+            cols = slice(i * N, (i + 1) * N)
+            nc.vector.tensor_copy(grouped[0][:, cols, :], w_raw[i][:, 0].rearrange("p j n -> p n j"))
+            nc.scalar.copy(grouped[1][:, cols, :], w_raw[i][:, 1].rearrange("p j n -> p n j"))
+            for g in range(PASSES):
+                nc.vector.quantize_mx(
+                    out=w_codes[g][:, cols].bitcast(FP8X4),
+                    scales=w_scales[g][:, cols],
+                    in_=grouped[g][:, cols, :].rearrange("p n j -> p (n j)"),
+                )
 
-        picked0 = keep.tile([P, S], U32, name="picked0", align_bytes=64)
-        nc.vector.tensor_copy(picked0[:], table[0][:].indirect(offs_t[:]))
         nc.vector.tensor_copy(x_picked_scales[:], table_scales[:].indirect(offs_t[:]))
+        quantise_w(0)
+        quantise_w(1)
 
         cols_ps = psum.tile([P, P], F32, name="cols_ps", tag="turned_ps10")
         nc.tensor.transpose(cols_ps[:], rows[:], ident[:])
@@ -127,55 +111,59 @@ def tile_picked_yharq_put_p_kernel(
         nc.scalar.activation(sent10[:], cols_ps[:, 0:BLOCKS], ACT.Copy, scale=10.0)
         nc.scalar.activation(cap_col[:], cols_ps[:, BLOCKS : 2 * BLOCKS], ACT.Relu, scale=2.0)
 
+        def spread_lim(dst, b, start, stop):
+            nc.tensor.matmul(
+                dst, lim_col[:, b : b + 1].to_broadcast([P, P]), ident[:], start=start, stop=stop, is_transpose=True
+            )
+
+        lim_ps = psum.tile([P, S], F32, name="lim_ps", tag="turned_ps11")
+        for b in range(BLOCKS):
+            spread_lim(lim_ps[:, block(b)], b, True, True)
+        cap = keep.tile([P, S], F32, name="cap")
+        neg_lim = keep.tile([P, S], F32, name="neg_lim")
+        abs_lim = keep.tile([P, S], F32, name="abs_lim")
+        nc.scalar.activation(cap[:], lim_ps[:], ACT.Relu, scale=2.0)
+        nc.scalar.activation(neg_lim[:], lim_ps[:], ACT.Copy, scale=-1.0)
+        nc.scalar.activation(abs_lim[:], lim_ps[:], ACT.Abs)
+
         turned_ps = {}
         for h in range(STREAM_TILES):
             for u in range(PARTS):
                 turned_ps[h, u] = psum.tile([P, PART], F32, name=f"turned_ps{h}{u}", tag=f"turned_ps{h}{u}")
         for u in range(PARTS):
             for i in range(PART_BLOCKS):
-                b = PART_BLOCKS * u + i
-                nc.tensor.matmul(
-                    turned_ps[0, u][:, block(i)],
-                    lim_col[:, b : b + 1].to_broadcast([P, P]),
-                    ident[:],
-                    start=(i == 0),
-                    stop=False,
-                    is_transpose=True,
-                )
+                spread_lim(turned_ps[0, u][:, block(i)], PART_BLOCKS * u + i, i == 0, False)
 
         acc = [psum.tile([P, 2 * N], F32, name=f"acc{b}", tag=f"acc{b}") for b in range(BLOCKS)]
 
-        def product(g, b, words):
-            nc.tensor.matmul_mx(
-                out=acc[b][:],
-                lhsT=words.bitcast(FP8X4),
-                lhsT_scale=x_picked_scales[SCALE_ROWS * g : P, block(b)],
-                rhs=w_codes[g][:].bitcast(FP8X4),
-                rhs_scale=w_scales[SCALE_ROWS * g : P, :],
-                start=(g == 0),
-                stop=(g == PASSES - 1),
-            )
-
-        quantise_w(0)
-        for b in range(PART_BLOCKS):
-            product(0, b, picked0[:, block(b)])
-        quantise_w(1)
-        for b in range(PART_BLOCKS, BLOCKS):
-            product(0, b, picked0[:, block(b)])
-        for u in range(PARTS):
-            picked1 = reuse.tile(
-                [P, PART], U32, name=f"picked1{u}", align_bytes=64, offset=AT_GROUPED + grouped_bytes + u * PART * 4
-            )
-            nc.vector.tensor_copy(picked1[:], table[1][:].indirect(offs_t[:, list_part(u)]))
-            for i in range(PART_BLOCKS):
-                product(1, PART_BLOCKS * u + i, picked1[:, block(i)])
+        for g in range(PASSES):
+            for u in range(PARTS):
+                picked = reuse.tile(
+                    [P, PART],
+                    U32,
+                    name=f"picked{g}{u}",
+                    align_bytes=64,
+                    offset=(PASSES - 1) * grouped_bytes + (PARTS * g + u) * PART * 4,
+                )
+                nc.vector.tensor_copy(picked[:], table[g][:].indirect(offs_t[:, list_part(u)]))
+                for i in range(PART_BLOCKS):
+                    b = PART_BLOCKS * u + i
+                    nc.tensor.matmul_mx(
+                        out=acc[b][:],
+                        lhsT=picked[:, block(i)].bitcast(FP8X4),
+                        lhsT_scale=x_picked_scales[SCALE_ROWS * g : P, block(b)],
+                        rhs=w_codes[g][:].bitcast(FP8X4),
+                        rhs_scale=w_scales[g][:],
+                        start=(g == 0),
+                        stop=(g == PASSES - 1),
+                    )
 
         turned = {}
         for u in range(PARTS):
             llr = []
             for i in range(PART_BLOCKS):
                 b = PART_BLOCKS * u + i
-                llr.append(reuse.tile([P, N], F32, name=f"llr{b}", offset=AT_LLR + b * KIB))
+                llr.append(keep.tile([P, N], F32, name=f"llr{b}"))
                 nc.scalar.activation(gain[b][:], acc[b][:, N : 2 * N], ACT.Sigmoid, bias=-math.log(6.0))
                 nc.vector.scalar_tensor_tensor(
                     llr[i][:], acc[b][:, 0:N], sent10[:, b : b + 1], gain[b][:], ALU.mult, ALU.mult
@@ -191,15 +179,8 @@ def tile_picked_yharq_put_p_kernel(
                         stop=not onto_lim or i == PART_BLOCKS - 1,
                         is_transpose=True,
                     )
-                turned[h, u] = reuse.tile(
-                    [P, PART], F32, name=f"turned{h}{u}", offset=AT_TURNED + (STREAM_TILES * u + h) * KIB
-                )
+                turned[h, u] = keep.tile([P, PART], F32, name=f"turned{h}{u}")
                 nc.scalar.copy(turned[h, u][:], turned_ps[h, u][:])
-
-        neg_lim = reuse.tile([P, S], F32, name="neg_lim", offset=AT_LLR)
-        nc.scalar.activation(neg_lim[:], lim_t[:], ACT.Copy, scale=-1.0)
-        cap = reuse.tile([P, S], F32, name="cap", offset=AT_LLR + PART_BLOCKS * KIB)
-        nc.scalar.activation(cap[:], lim_t[:], ACT.Relu, scale=2.0)
 
         comb0 = keep.tile([P, S], F32, name="comb0")
         under = keep.tile([P, BLOCKS, P], F32, name="under")
@@ -214,7 +195,7 @@ def tile_picked_yharq_put_p_kernel(
             )
             nc.vector.tensor_tensor(comb1[:], window[1][:].indirect(slot_t[:, list_part(u)]), turned[1, u][:], ALU.add)
             comb1_ps = psum.tile([P, PART], F32, name=f"comb1_ps{u}", tag=f"acc{u}")
-            above = reuse.tile([P, PART_BLOCKS, P], F32, name=f"above{u}", offset=AT_LIM + u * KIB)
+            above = keep.tile([P, PART_BLOCKS, P], F32, name=f"above{u}")
             for i in range(PART_BLOCKS):
                 nc.tensor.transpose(comb1_ps[:, block(i)], comb1[:, block(i)], ident[:])
             for i in range(PART_BLOCKS):
@@ -226,8 +207,6 @@ def tile_picked_yharq_put_p_kernel(
                     under[:, b, :], above[:, i, :], ACT.Relu, bias=cap_col[:, b : b + 1], scale=-1.0
                 )
                 nc.tensor.transpose(under_ps[:, block(b)], under[:, b, :], ident[:])
-        abs_lim = reuse.tile([P, S], F32, name="abs_lim", offset=AT_TURNED + STREAM_TILES * KIB)
-        nc.scalar.activation(abs_lim[:], neg_lim[:], ACT.Abs)
         neg_under = keep.tile([P, S], F32, name="neg_under")
         nc.scalar.activation(neg_under[:], under_ps[:], ACT.Copy, scale=-1.0)
 

import math
from contextlib import ExitStack

import concourse.mybir as mybir
from concourse.masks import make_identity

K, T, S, N, U = 1024, 2048, 512, 256, 1024
FLOPS = 2 * 2 * K * N * S

F32 = mybir.dt.float32
BF16 = mybir.dt.bfloat16
I32 = mybir.dt.int32
U32 = mybir.dt.uint32
U16 = mybir.dt.uint16
U8 = mybir.dt.uint8
FP8X4 = mybir.dt.float8_e4m3fn_x4
ALU = mybir.AluOpType
ACT = mybir.ActivationFunctionType

P = 128
PACK = 4
PASSES = K // (P * PACK)
QUADRANT = 32
SCALE_ROWS = 4
BLOCKS = S // P
STREAM_TILES = N // P
PARTS = 2
PART = S // PARTS
PART_BLOCKS = BLOCKS // PARTS
PER_COL = 16


def tile_picked_yharq_put_p_kernel(
    tc, x_words, x_scales, w1, w2, buf, sent, lim, offs, slot, out
):
    nc = tc.nc
    with ExitStack() as ctx:
        keep = ctx.enter_context(tc.tile_pool(name="keep", bufs=1))
        reuse = ctx.enter_context(tc.tile_pool(name="reuse", bufs=1))
        psum = ctx.enter_context(tc.psum_pool(name="psum", bufs=1))

        def block(b):
            return slice(b * P, (b + 1) * P)

        def list_part(u):
            return slice(u * PART // PER_COL, (u + 1) * PART // PER_COL)

        offs_t = keep.tile([P, S // PER_COL], U16, name="offs_t")
        slot_t = keep.tile([P, S // PER_COL], U16, name="slot_t")
        table_scales = keep.tile([P, T], U8, name="table_scales", align_bytes=64)
        rows = keep.tile([P, P], F32, name="rows")
        ident = keep.tile([P, P], F32, name="ident")
        gain = [keep.tile([P, N], F32, name=f"gain{b}") for b in range(BLOCKS)]
        w_raw = [keep.tile([P, PASSES, PACK, N], F32, name=f"w_raw{i}") for i in range(2)]
        table = [keep.tile([P, T], U32, name=f"table{g}", align_bytes=64) for g in range(PASSES)]
        window = [keep.tile([P, U], F32, name=f"window{h}", align_bytes=64) for h in range(STREAM_TILES)]

        nc.vector.memset(table_scales[:].bitcast(I32), 0)
        nc.gpsimd.memset(rows[:], 0.0)
        make_identity(nc, ident[:])

        def load_w(i, w):
            nc.sync.dma_start(w_raw[i][:], w.rearrange("(g p j) n -> p g j n", g=PASSES, j=PACK))

        load_w(0, w1)
        nc.sync.dma_start(offs_t[:], offs)
        for q in range(P // QUADRANT):
            nc.sync.dma_start(
                table_scales[QUADRANT * q : QUADRANT * q + SCALE_ROWS * PASSES, :].bitcast(I32),
                x_scales[:, SCALE_ROWS * q : SCALE_ROWS * (q + 1), :].bitcast(I32),
            )
        load_w(1, w2)
        nc.sync.dma_start(rows[0:BLOCKS, :], sent[0, :].rearrange("(b c) -> b c", b=BLOCKS))
        nc.sync.dma_start(rows[BLOCKS : 2 * BLOCKS, :], lim[0, :].rearrange("(b c) -> b c", b=BLOCKS))
        for g in range(PASSES):
            nc.sync.dma_start(table[g][:].bitcast(I32), x_words[g].rearrange("p c r -> p (c r)").bitcast(I32))
        nc.sync.dma_start(slot_t[:], slot)
        for h in range(STREAM_TILES):
            nc.sync.dma_start(window[h][:], buf[block(h), :])

        w_codes = [keep.tile([P, 2 * N], U32, name=f"w_codes{g}", align_bytes=64) for g in range(PASSES)]
        w_scales = [keep.tile([P, 2 * N], U8, name=f"w_scales{g}", align_bytes=64) for g in range(PASSES)]
        x_picked_scales = keep.tile([P, S], U8, name="x_picked_scales", align_bytes=64)
        grouped_bytes = 2 * N * PACK * 2
        grouped = [
            reuse.tile([P, 2 * N, PACK], BF16, name=f"grouped{g}", align_bytes=64, offset=g * grouped_bytes)
            for g in range(PASSES)
        ]

        def quantise_w(i):
            cols = slice(i * N, (i + 1) * N)
            nc.vector.tensor_copy(grouped[0][:, cols, :], w_raw[i][:, 0].rearrange("p j n -> p n j"))
            nc.scalar.copy(grouped[1][:, cols, :], w_raw[i][:, 1].rearrange("p j n -> p n j"))
            for g in range(PASSES):
                nc.vector.quantize_mx(
                    out=w_codes[g][:, cols].bitcast(FP8X4),
                    scales=w_scales[g][:, cols],
                    in_=grouped[g][:, cols, :].rearrange("p n j -> p (n j)"),
                )

        nc.vector.tensor_copy(x_picked_scales[:], table_scales[:].indirect(offs_t[:]))
        quantise_w(0)
        quantise_w(1)

        cols_ps = psum.tile([P, P], F32, name="cols_ps", tag="turned_ps10")
        nc.tensor.transpose(cols_ps[:], rows[:], ident[:])
        sent10 = keep.tile([P, BLOCKS], F32, name="sent10")
        lim_col = keep.tile([P, BLOCKS], F32, name="lim_col")
        cap_col = keep.tile([P, BLOCKS], F32, name="cap_col")
        nc.scalar.copy(lim_col[:], cols_ps[:, BLOCKS : 2 * BLOCKS])
        nc.scalar.activation(sent10[:], cols_ps[:, 0:BLOCKS], ACT.Copy, scale=10.0)
        nc.scalar.activation(cap_col[:], cols_ps[:, BLOCKS : 2 * BLOCKS], ACT.Relu, scale=2.0)

        def spread_lim(dst, b, start, stop):
            nc.tensor.matmul(
                dst, lim_col[:, b : b + 1].to_broadcast([P, P]), ident[:], start=start, stop=stop, is_transpose=True
            )

        lim_ps = psum.tile([P, S], F32, name="lim_ps", tag="turned_ps11")
        for b in range(BLOCKS):
            spread_lim(lim_ps[:, block(b)], b, True, True)
        cap = keep.tile([P, S], F32, name="cap")
        neg_lim = keep.tile([P, S], F32, name="neg_lim")
        abs_lim = keep.tile([P, S], F32, name="abs_lim")
        nc.scalar.activation(cap[:], lim_ps[:], ACT.Relu, scale=2.0)
        nc.scalar.activation(neg_lim[:], lim_ps[:], ACT.Copy, scale=-1.0)
        nc.scalar.activation(abs_lim[:], lim_ps[:], ACT.Abs)

        turned_ps = {}
        for h in range(STREAM_TILES):
            for u in range(PARTS):
                turned_ps[h, u] = psum.tile([P, PART], F32, name=f"turned_ps{h}{u}", tag=f"turned_ps{h}{u}")
        for u in range(PARTS):
            for i in range(PART_BLOCKS):
                spread_lim(turned_ps[0, u][:, block(i)], PART_BLOCKS * u + i, i == 0, False)

        acc = [psum.tile([P, 2 * N], F32, name=f"acc{b}", tag=f"acc{b}") for b in range(BLOCKS)]

        for g in range(PASSES):
            for u in range(PARTS):
                picked = reuse.tile(
                    [P, PART],
                    U32,
                    name=f"picked{g}{u}",
                    align_bytes=64,
                    offset=(PASSES - 1) * grouped_bytes + (PARTS * g + u) * PART * 4,
                )
                nc.vector.tensor_copy(picked[:], table[g][:].indirect(offs_t[:, list_part(u)]))
                for i in range(PART_BLOCKS):
                    b = PART_BLOCKS * u + i
                    nc.tensor.matmul_mx(
                        out=acc[b][:],
                        lhsT=picked[:, block(i)].bitcast(FP8X4),
                        lhsT_scale=x_picked_scales[SCALE_ROWS * g : P, block(b)],
                        rhs=w_codes[g][:].bitcast(FP8X4),
                        rhs_scale=w_scales[g][:],
                        start=(g == 0),
                        stop=(g == PASSES - 1),
                    )

        turned = {}
        for u in range(PARTS):
            llr = []
            for i in range(PART_BLOCKS):
                b = PART_BLOCKS * u + i
                llr.append(keep.tile([P, N], F32, name=f"llr{b}"))
                nc.scalar.activation(gain[b][:], acc[b][:, N : 2 * N], ACT.Sigmoid, bias=-math.log(6.0))
                nc.vector.scalar_tensor_tensor(
                    llr[i][:], acc[b][:, 0:N], sent10[:, b : b + 1], gain[b][:], ALU.mult, ALU.mult
                )
            for h in range(STREAM_TILES):
                onto_lim = h == 0
                for i in range(PART_BLOCKS):
                    nc.tensor.matmul(
                        turned_ps[h, u][:, block(i)],
                        llr[i][:, block(h)],
                        ident[:],
                        start=not onto_lim,
                        stop=not onto_lim or i == PART_BLOCKS - 1,
                        is_transpose=True,
                    )
                turned[h, u] = keep.tile([P, PART], F32, name=f"turned{h}{u}")
                nc.scalar.copy(turned[h, u][:], turned_ps[h, u][:])

        comb0 = keep.tile([P, S], F32, name="comb0")
        under = keep.tile([P, BLOCKS, P], F32, name="under")
        under_ps = psum.tile([P, S], F32, name="under_ps", tag="acc2")
        for u in range(PARTS):
            comb1 = keep.tile([P, PART], F32, name=f"comb1{u}")
            nc.vector.tensor_tensor(
                comb0[:, u * PART : (u + 1) * PART],
                window[0][:].indirect(slot_t[:, list_part(u)]),
                turned[0, u][:],
                ALU.add,
            )
            nc.vector.tensor_tensor(comb1[:], window[1][:].indirect(slot_t[:, list_part(u)]), turned[1, u][:], ALU.add)
            comb1_ps = psum.tile([P, PART], F32, name=f"comb1_ps{u}", tag=f"acc{u}")
            above = keep.tile([P, PART_BLOCKS, P], F32, name=f"above{u}")
            for i in range(PART_BLOCKS):
                nc.tensor.transpose(comb1_ps[:, block(i)], comb1[:, block(i)], ident[:])
            for i in range(PART_BLOCKS):
                b = PART_BLOCKS * u + i
                nc.scalar.activation(above[:, i, :], comb1_ps[:, block(i)], ACT.Relu, bias=lim_col[:, b : b + 1])
            for i in range(PART_BLOCKS):
                b = PART_BLOCKS * u + i
                nc.scalar.activation(
                    under[:, b, :], above[:, i, :], ACT.Relu, bias=cap_col[:, b : b + 1], scale=-1.0
                )
                nc.tensor.transpose(under_ps[:, block(b)], under[:, b, :], ident[:])
        neg_under = keep.tile([P, S], F32, name="neg_under")
        nc.scalar.activation(neg_under[:], under_ps[:], ACT.Copy, scale=-1.0)

        capped0 = keep.tile([P, S], F32, name="capped0")
        nc.vector.scalar_tensor_tensor(capped0[:], comb0[:], 0.0, cap[:], ALU.max, ALU.min)
        nc.vector.tensor_tensor(window[0][:].indirect(slot_t[:]), capped0[:], neg_lim[:], ALU.add)
        nc.sync.dma_start(out[block(0), :], window[0][:])
        nc.vector.tensor_tensor(window[1][:].indirect(slot_t[:]), neg_under[:], abs_lim[:], ALU.add)
        nc.sync.dma_start(out[block(1), :], window[1][:])
